import numpy as np
import ml_dtypes


def mxq(x, axis, fmt="e4m3"):
    dtype, down = {"e4m3": (ml_dtypes.float8_e4m3fn, 7), "e5m2": (ml_dtypes.float8_e5m2, 14)}[fmt]
    v = np.moveaxis(np.asarray(x, np.float32).astype(ml_dtypes.bfloat16).astype(np.float64), axis, -1)
    blocks = v.reshape(v.shape[:-1] + (-1, 32))
    amax = np.abs(blocks).max(-1, keepdims=True)
    byte = np.maximum(np.where(amax > 0, np.frexp(amax)[1] - 1 + 127, 0) - down, 1)
    scale = np.exp2(byte - 127.0)
    codes = (blocks / scale).astype(np.float32).astype(dtype).astype(np.float64)
    return np.moveaxis((codes * scale).reshape(v.shape), -1, axis)


WIDE = False


def mx_kscale(k, group=512):
    if not WIDE:
        return np.ones(k)
    levels = np.array([10, -10, 5, -5, 0])
    if group != 512:
        return np.exp2(np.random.permutation(np.resize(levels, k // group))).repeat(group)
    if k % 512:
        return np.exp2(np.random.permutation(np.resize(levels, k // 32))).repeat(32)
    a = np.empty((k // 512, 16))
    for p in range(k // 512):
        a[p, :8] = np.random.permutation(np.resize(levels, 8))
        for g in range(8):
            far = levels[np.abs(levels - a[p, g]) >= 10]
            a[p, g + 8] = far[np.random.randint(len(far))]
    return np.exp2(a.ravel()).repeat(32)


def f64(x):
    return np.asarray(x).astype(np.float64)


def striped(idx):
    return np.tile(np.asarray(idx).reshape(-1, 16).T, (8, 1)).astype(np.uint16)


def unstriped(offs):
    return offs[:16].T.reshape(-1).astype(np.int64)


H, KV, D, NQ, N = 4, 1, 256, 512, 512


def setup_inputs():
    n = np.random.standard_normal
    s = mx_kscale(D, 0)[:, None]
    u = mx_kscale(N)
    t = np.random.uniform(0.5, 2.0, N) * u
    v = n((KV, N, 128))
    return {
        "qT": (n((H, D, NQ)) * s * (0.70 / np.sqrt(D))).astype(np.float32),
        "kT": (n((KV, D, N)) / s).astype(np.float32),
        "t": t.reshape(N, 1).astype(np.float32),
        "v": (v / t[:, None]).astype(np.float32),
        "kb": (0.5 * n((N, 1))).astype(np.float32),
        "mask": np.exp2(-np.abs(np.arange(NQ)[None, :] * N / NQ - np.arange(N)[:, None]) / 256.0).astype(np.float32),
        "og": n((H, NQ, 128)).astype(np.float32),
    }


def reference(qT, kT, t, v, kb, mask, og):
    a = np.repeat(mxq(f64(kT), 1, "e4m3"), H // KV, 0).transpose(0, 2, 1) @ mxq(f64(qT), 1, "e4m3")
    a = a + f64(kb)
    p = a
    p = p * f64(mask)
    w = p * f64(t)
    y = mxq(w, 1, "e4m3").transpose(0, 2, 1) @ np.repeat(mxq(f64(v), 1, "e4m3"), H // KV, 0)
    y = y / 16.0
    y = y / (1.0 + np.exp(-f64(og)))
    return y

@@ -1,0 +1,295 @@
+from contextlib import ExitStack
+
+import concourse.mybir as mybir
+
+H, D, NQ, N, E = 4, 256, 512, 512, 128
+FLOPS = 2 * H * N * NQ * D + 2 * H * NQ * N * E
+
+F32 = mybir.dt.float32
+BF16 = mybir.dt.bfloat16
+U32 = mybir.dt.uint32
+I32 = mybir.dt.int32
+U8 = mybir.dt.uint8
+FP8X4 = mybir.dt.float8_e4m3fn_x4
+ACT = mybir.ActivationFunctionType
+ALU = mybir.AluOpType
+
+P = 128
+PACK = 4
+ROWS = D // PACK
+COLS = 128
+HALF = 256
+RUN = 4
+
+
+def tile_rows_a_lin_kb_mask_gate_kernel(tc, qT, kT, t, v, kb, mask, og, out):
+    nc = tc.nc
+    with ExitStack() as ctx:
+        sb = ctx.enter_context(tc.tile_pool(name="sb", bufs=1))
+        score_psum = ctx.enter_context(tc.psum_pool(name="score_psum", bufs=3))
+        y_psum = ctx.enter_context(tc.psum_pool(name="y_psum", bufs=2))
+        ctx.enter_context(tc.manual_schedule())
+
+        def new(name, shape, dtype):
+            return sb.tile(shape, dtype, name=name, align_bytes=64)
+
+        t_sb = new("t_sb", [P, PACK], F32)
+        kb_sb = new("kb_sb", [P, PACK], F32)
+        kbt = new("kbt", [P, PACK], F32)
+        k_raw = new("k_raw", [P, PACK, N], F32)
+        k_bf = [new("k_bf%d" % i, [P, 2, COLS, PACK], BF16) for i in range(2)]
+        k_mx = new("k_mx", [P, N + N // 4], U32)
+        k_codes = k_mx[:, 0:N]
+        k_scales = k_mx[:, N : N + N // 4].bitcast(U8)
+        v_raw = new("v_raw", [P, PACK, E], F32)
+        v_bf = new("v_bf", [P, E, PACK], BF16)
+        v_codes = new("v_codes", [P, E], U32)
+        v_scales = new("v_scales", [P, E], U8)
+        parts = [(pair, u) for pair in range(2) for u in range(2)]
+        q_raw = {(0, u): new("q_raw0%d" % u, [P, PACK, HALF], F32)[:] for u in range(2)}
+        q_raw_late = new("q_raw_late", [P, PACK, NQ], F32)
+        for u in range(2):
+            q_raw[1, u] = q_raw_late[:, :, u * HALF : (u + 1) * HALF]
+        q_bf = {x: new("q_bf%d%d" % x, [P, HALF, PACK], BF16) for x in parts}
+        q_codes = {x: new("q_codes%d%d" % x, [P, HALF], U32) for x in parts}
+        q_scales = {x: new("q_scales%d%d" % x, [P, HALF], U8) for x in parts}
+        mask_sb = [new("mask_sb%d" % u, [P, PACK, HALF], F32) for u in range(2)]
+        og_sb = [new("og_sb%d" % pair, [P, 2, NQ // COLS, E], F32) for pair in range(2)]
+        gate = [new("gate%d" % h, [P, NQ // COLS, E], F32) for h in range(H)]
+
+        units = [(0, 0), (0, 1), (1, 0), (1, 1), (2, 0), (3, 0), (2, 1), (3, 1)]
+        a_sb = [new("a_sb%d" % n, [P, PACK, HALF], F32) for n in range(len(units))]
+        w_bf = [new("w_bf%d" % n, [P, HALF, PACK], BF16) for n in range(len(units))]
+        w_codes = [new("w_codes%d" % n, [P, HALF], U32) for n in range(len(units))]
+        w_scales = [new("w_scales%d" % n, [P, HALF], U8) for n in range(len(units))]
+        o_sb = [new("o_sb%d" % n, [P, 2, E], F32) for n in range(len(units))]
+        banks = {}
+        y_bank = {}
+
+        def runs_of_rows(ap):
+            return ap.rearrange("p j (n i) -> p n j i", i=RUN)
+
+        def runs_of_words(ap):
+            return ap.rearrange("p (n i) j -> p n j i", i=RUN)
+
+        def quantize(codes, scales, words):
+            nc.vector.quantize_mx(out=codes.bitcast(FP8X4), scales=scales, in_=words)
+
+        def q_rows(pair):
+            return qT[2 * pair : 2 * pair + 2].rearrange("g (p j) n -> (g p) j n", j=PACK)
+
+        def load_mask(u):
+            rows = mask.rearrange("(p r) n -> p r n", r=PACK)
+            nc.sync.dma_start(out=mask_sb[u][:], in_=rows[:, :, u * HALF : (u + 1) * HALF])
+
+        def load_og(pair):
+            rows = og[2 * pair : 2 * pair + 2].rearrange("g (c m) e -> m (g c) e", m=COLS)
+            nc.sync.dma_start(out=og_sb[pair][:].rearrange("p g c e -> p (g c) e"), in_=rows)
+
+        def round_on_vector(dst, src):
+            nc.vector.tensor_copy(out=dst, in_=src)
+
+        def round_on_scalar(dst, src):
+            nc.scalar.activation(out=dst, in_=src, func=ACT.Copy)
+
+        def round_k(rounder, i):
+            src = k_raw[0:ROWS].rearrange("p j (m r) -> p m j r", r=PACK)[:, :, :, 2 * i : 2 * i + 2]
+            rounder(k_bf[i][0:ROWS].rearrange("p r m j -> p m j r"), src)
+
+        def quantize_k(r):
+            cols = slice(r * COLS, (r + 1) * COLS)
+            words = k_bf[r // 2][0:ROWS, r % 2].rearrange("p m j -> p (m j)")
+            quantize(k_codes[0:ROWS, cols], k_scales[0:ROWS, cols], words)
+
+        def round_q(rounder, x, cols=slice(0, HALF)):
+            rounder(runs_of_words(q_bf[x][:, cols, :]), runs_of_rows(q_raw[x][:, :, cols]))
+
+        def quantize_q(x, cols=slice(0, HALF)):
+            quantize(q_codes[x][:, cols], q_scales[x][:, cols], q_bf[x][:, cols, :].rearrange("p n j -> p (n j)"))
+
+        def scores(n):
+            h, u = units[n]
+            g = h % 2
+            rows = slice(g * ROWS, (g + 1) * ROWS)
+            x = (h // 2, u)
+            for i in range(2):
+                bank = score_psum.tile([P, 2, HALF], F32, name="scores_of_tile%d" % g)
+                banks[n, i] = bank
+                for r in range(2 * i, 2 * i + 2):
+                    tokens = slice(r * COLS, (r + 1) * COLS)
+                    for c in range(2):
+                        cols = slice(c * COLS, (c + 1) * COLS)
+                        nc.tensor.matmul_mx(
+                            out=bank[:, r % 2, cols],
+                            lhsT=k_codes[rows, tokens].bitcast(FP8X4),
+                            lhsT_scale=k_scales[rows, tokens],
+                            rhs=q_codes[x][rows, cols].bitcast(FP8X4),
+                            rhs_scale=q_scales[x][rows, cols],
+                            start=True,
+                            stop=True,
+                        )
+
+        def bias_and_scale_on_vector(n, places):
+            for r in places:
+                nc.vector.tensor_scalar(
+                    out=a_sb[n][:, r, :],
+                    in0=banks[n, r // 2][:, r % 2, :],
+                    scalar1=t_sb[:, r : r + 1],
+                    scalar2=kbt[:, r : r + 1],
+                    op0=ALU.mult,
+                    op1=ALU.add,
+                )
+
+        def bias_and_scale(n, places=range(PACK)):
+            for r in places:
+                nc.scalar.activation(
+                    out=a_sb[n][:, r, :],
+                    in_=banks[n, r // 2][:, r % 2, :],
+                    func=ACT.Identity,
+                    bias=kbt[:, r : r + 1],
+                    scale=t_sb[:, r : r + 1],
+                )
+
+        def decay(n):
+            u = units[n][1]
+            nc.vector.tensor_tensor(
+                out=runs_of_words(w_bf[n][:]),
+                in0=runs_of_rows(a_sb[n][:]),
+                in1=runs_of_rows(mask_sb[u][:]),
+                op=ALU.mult,
+            )
+
+        def quantize_w(n):
+            quantize(w_codes[n][:], w_scales[n][:], w_bf[n][:].rearrange("p n r -> p (n r)"))
+
+        def values(n):
+            h, u = units[n]
+            if u == 0:
+                y_bank[h] = y_psum.tile([P, NQ // COLS, E], F32, name="y_bank")
+            for c in range(2):
+                cols = slice(c * COLS, (c + 1) * COLS)
+                nc.tensor.matmul_mx(
+                    out=y_bank[h][:, 2 * u + c, :],
+                    lhsT=w_codes[n][:, cols].bitcast(FP8X4),
+                    lhsT_scale=w_scales[n][:, cols],
+                    rhs=v_codes[:].bitcast(FP8X4),
+                    rhs_scale=v_scales[:],
+                    start=True,
+                    stop=True,
+                )
+
+        def gate_tanh(h):
+            nc.scalar.activation(out=gate[h][:], in_=og_sb[h // 2][:, h % 2], func=ACT.Tanh, scale=0.5)
+
+        def finish(n):
+            h, u = units[n]
+            tiles = slice(2 * u, 2 * u + 2)
+            nc.vector.scalar_tensor_tensor(
+                out=o_sb[n][:],
+                in0=gate[h][:, tiles, :],
+                scalar=1.0,
+                in1=y_bank[h][:, tiles, :],
+                op0=ALU.add,
+                op1=ALU.mult,
+            )
+            rows = out[h].rearrange("(c m) e -> m c e", m=COLS)
+            nc.sync.dma_start(out=rows[:, tiles, :], in_=o_sb[n][:])
+
+        first, second = slice(0, COLS), slice(COLS, HALF)
+
+        nc.sync.dma_start(out=k_raw[0:ROWS], in_=kT[0].rearrange("(p j) n -> p j n", j=PACK))
+        nc.scalar.dma_start(out=t_sb[:], in_=t.rearrange("(p r) o -> p (r o)", r=PACK))
+        nc.scalar.dma_start(out=kb_sb[:], in_=kb.rearrange("(p r) o -> p (r o)", r=PACK))
+        nc.sync.dma_start(out=q_raw[0, 0], in_=q_rows(0)[:, :, 0:HALF])
+        nc.sync.dma_start(out=q_raw[0, 1], in_=q_rows(0)[:, :, HALF:NQ])
+        load_mask(0)
+        nc.sync.dma_start(out=v_raw[:], in_=v[0].rearrange("(p j) e -> p j e", j=PACK))
+        load_mask(1)
+
+        nc.vector.memset(k_mx[:, N : N + N // 4], 0)
+        round_k(round_on_vector, 0)
+        round_k(round_on_scalar, 1)
+        nc.vector.tensor_tensor(out=kbt[:], in0=kb_sb[:], in1=t_sb[:], op=ALU.mult)
+        quantize_k(0)
+        quantize_k(1)
+        round_q(round_on_vector, (0, 0), first)
+        round_q(round_on_scalar, (0, 0), second)
+        quantize_k(2)
+        quantize_k(3)
+        nc.scalar.dma_start(out=k_mx[ROWS:P, :].bitcast(I32), in_=k_mx[0:ROWS, :].bitcast(I32))
+        nc.sync.dma_start(out=q_raw_late[:], in_=q_rows(1))
+        load_og(0)
+        load_og(1)
+
+        quantize_q((0, 0), first)
+        quantize_q((0, 0), second)
+        scores(0)
+        round_q(round_on_vector, (0, 1))
+        bias_and_scale(0, (0, 1))
+        bias_and_scale_on_vector(0, (2,))
+        quantize_q((0, 1))
+        bias_and_scale_on_vector(0, (3,))
+        scores(1)
+        nc.vector.tensor_scalar_mul(runs_of_words(v_bf[:]), runs_of_rows(v_raw[:]), 1.0 / 32.0)
+
+        bias_and_scale(1)
+        decay(0)
+        quantize(v_codes[:], v_scales[:], v_bf[:].rearrange("p e j -> p (e j)"))
+        scores(2)
+
+        bias_and_scale(2)
+        decay(1)
+        scores(3)
+        quantize_w(0)
+        values(0)
+
+        bias_and_scale(3)
+        round_q(round_on_vector, (1, 0))
+        round_q(round_on_scalar, (1, 1))
+        gate_tanh(0)
+        decay(2)
+        quantize_q((1, 0))
+        scores(4)
+        quantize_w(1)
+        values(1)
+
+        bias_and_scale(4)
+        decay(3)
+        quantize_q((1, 1))
+        scores(5)
+        quantize_w(2)
+        values(2)
+        finish(0)
+
+        bias_and_scale(5)
+        gate_tanh(1)
+        decay(4)
+        scores(6)
+        quantize_w(3)
+        values(3)
+        finish(1)
+
+        bias_and_scale(6)
+        decay(5)
+        scores(7)
+        quantize_w(4)
+        values(4)
+        finish(2)
+        finish(3)
+
+        bias_and_scale(7)
+        gate_tanh(3)
+        gate_tanh(2)
+        decay(6)
+        quantize_w(5)
+        values(5)
+
+        decay(7)
+        quantize_w(6)
+        values(6)
+        finish(5)
+        quantize_w(7)
+        values(7)
+        finish(4)
+        finish(6)
+        finish(7)

@@ -19,7 +19,7 @@ PACK = 4
 ROWS = D // PACK
 COLS = 128
 HALF = 256
-RUN = 4
+RUN = 2
 
 
 def tile_rows_a_lin_kb_mask_gate_kernel(tc, qT, kT, t, v, kb, mask, og, out):
@@ -53,7 +53,7 @@ def tile_rows_a_lin_kb_mask_gate_kernel(tc, qT, kT, t, v, kb, mask, og, out):
         q_bf = {x: new("q_bf%d%d" % x, [P, HALF, PACK], BF16) for x in parts}
         q_codes = {x: new("q_codes%d%d" % x, [P, HALF], U32) for x in parts}
         q_scales = {x: new("q_scales%d%d" % x, [P, HALF], U8) for x in parts}
-        mask_sb = [new("mask_sb%d" % u, [P, PACK, HALF], F32) for u in range(2)]
+        mask_sb = new("mask_sb", [P, PACK, NQ], F32)
         og_sb = [new("og_sb%d" % pair, [P, 2, NQ // COLS, E], F32) for pair in range(2)]
         gate = [new("gate%d" % h, [P, NQ // COLS, E], F32) for h in range(H)]
 
@@ -77,10 +77,6 @@ def tile_rows_a_lin_kb_mask_gate_kernel(tc, qT, kT, t, v, kb, mask, og, out):
 
         def q_rows(pair):
             return qT[2 * pair : 2 * pair + 2].rearrange("g (p j) n -> (g p) j n", j=PACK)
-
-        def load_mask(u):
-            rows = mask.rearrange("(p r) n -> p r n", r=PACK)
-            nc.sync.dma_start(out=mask_sb[u][:], in_=rows[:, :, u * HALF : (u + 1) * HALF])
 
         def load_og(pair):
             rows = og[2 * pair : 2 * pair + 2].rearrange("g (c m) e -> m (g c) e", m=COLS)
@@ -129,19 +125,8 @@ def tile_rows_a_lin_kb_mask_gate_kernel(tc, qT, kT, t, v, kb, mask, og, out):
                             stop=True,
                         )
 
-        def bias_and_scale_on_vector(n, places):
-            for r in places:
-                nc.vector.tensor_scalar(
-                    out=a_sb[n][:, r, :],
-                    in0=banks[n, r // 2][:, r % 2, :],
-                    scalar1=t_sb[:, r : r + 1],
-                    scalar2=kbt[:, r : r + 1],
-                    op0=ALU.mult,
-                    op1=ALU.add,
-                )
-
-        def bias_and_scale(n, places=range(PACK)):
-            for r in places:
+        def bias_and_scale(n):
+            for r in range(PACK):
                 nc.scalar.activation(
                     out=a_sb[n][:, r, :],
                     in_=banks[n, r // 2][:, r % 2, :],
@@ -155,7 +140,7 @@ def tile_rows_a_lin_kb_mask_gate_kernel(tc, qT, kT, t, v, kb, mask, og, out):
             nc.vector.tensor_tensor(
                 out=runs_of_words(w_bf[n][:]),
                 in0=runs_of_rows(a_sb[n][:]),
-                in1=runs_of_rows(mask_sb[u][:]),
+                in1=runs_of_rows(mask_sb[:, :, u * HALF : (u + 1) * HALF]),
                 op=ALU.mult,
             )
 
@@ -202,9 +187,7 @@ def tile_rows_a_lin_kb_mask_gate_kernel(tc, qT, kT, t, v, kb, mask, og, out):
         nc.scalar.dma_start(out=kb_sb[:], in_=kb.rearrange("(p r) o -> p (r o)", r=PACK))
         nc.sync.dma_start(out=q_raw[0, 0], in_=q_rows(0)[:, :, 0:HALF])
         nc.sync.dma_start(out=q_raw[0, 1], in_=q_rows(0)[:, :, HALF:NQ])
-        load_mask(0)
-        nc.sync.dma_start(out=v_raw[:], in_=v[0].rearrange("(p j) e -> p j e", j=PACK))
-        load_mask(1)
+        nc.sync.dma_start(out=mask_sb[:], in_=mask.rearrange("(p r) n -> p r n", r=PACK))
 
         nc.vector.memset(k_mx[:, N : N + N // 4], 0)
         round_k(round_on_vector, 0)
@@ -216,8 +199,9 @@ def tile_rows_a_lin_kb_mask_gate_kernel(tc, qT, kT, t, v, kb, mask, og, out):
         round_q(round_on_scalar, (0, 0), second)
         quantize_k(2)
         quantize_k(3)
-        nc.scalar.dma_start(out=k_mx[ROWS:P, :].bitcast(I32), in_=k_mx[0:ROWS, :].bitcast(I32))
+        nc.sync.dma_start(out=k_mx[ROWS:P, :].bitcast(I32), in_=k_mx[0:ROWS, :].bitcast(I32))
         nc.sync.dma_start(out=q_raw_late[:], in_=q_rows(1))
+        nc.sync.dma_start(out=v_raw[:], in_=v[0].rearrange("(p j) e -> p j e", j=PACK))
         load_og(0)
         load_og(1)
 
@@ -225,65 +209,55 @@ def tile_rows_a_lin_kb_mask_gate_kernel(tc, qT, kT, t, v, kb, mask, og, out):
         quantize_q((0, 0), second)
         scores(0)
         round_q(round_on_vector, (0, 1))
-        bias_and_scale(0, (0, 1))
-        bias_and_scale_on_vector(0, (2,))
+        bias_and_scale(0)
         quantize_q((0, 1))
-        bias_and_scale_on_vector(0, (3,))
         scores(1)
-        nc.vector.tensor_scalar_mul(runs_of_words(v_bf[:]), runs_of_rows(v_raw[:]), 1.0 / 32.0)
-
         bias_and_scale(1)
         decay(0)
-        quantize(v_codes[:], v_scales[:], v_bf[:].rearrange("p e j -> p (e j)"))
         scores(2)
-
         bias_and_scale(2)
         decay(1)
         scores(3)
         quantize_w(0)
-        values(0)
-
+        round_q(round_on_scalar, (1, 0))
         bias_and_scale(3)
-        round_q(round_on_vector, (1, 0))
-        round_q(round_on_scalar, (1, 1))
-        gate_tanh(0)
         decay(2)
         quantize_q((1, 0))
         scores(4)
+        nc.vector.tensor_scalar_mul(runs_of_words(v_bf[:]), runs_of_rows(v_raw[:]), 1.0 / 32.0)
         quantize_w(1)
-        values(1)
-
+        round_q(round_on_scalar, (1, 1))
         bias_and_scale(4)
         decay(3)
-        quantize_q((1, 1))
+        quantize(v_codes[:], v_scales[:], v_bf[:].rearrange("p e j -> p (e j)"))
         scores(5)
+        values(0)
+        values(1)
+        quantize_q((1, 1))
         quantize_w(2)
         values(2)
-        finish(0)
-
+        gate_tanh(0)
         bias_and_scale(5)
-        gate_tanh(1)
         decay(4)
         scores(6)
+        finish(0)
         quantize_w(3)
         values(3)
         finish(1)
-
         bias_and_scale(6)
+        gate_tanh(1)
         decay(5)
         scores(7)
         quantize_w(4)
         values(4)
+        bias_and_scale(7)
+        decay(6)
         finish(2)
         finish(3)
-
-        bias_and_scale(7)
-        gate_tanh(3)
-        gate_tanh(2)
-        decay(6)
         quantize_w(5)
         values(5)
-
+        gate_tanh(3)
+        gate_tanh(2)
         decay(7)
         quantize_w(6)
         values(6)

@@ -53,11 +53,11 @@ def tile_rows_a_lin_kb_mask_gate_kernel(tc, qT, kT, t, v, kb, mask, og, out):
         q_bf = {x: new("q_bf%d%d" % x, [P, HALF, PACK], BF16) for x in parts}
         q_codes = {x: new("q_codes%d%d" % x, [P, HALF], U32) for x in parts}
         q_scales = {x: new("q_scales%d%d" % x, [P, HALF], U8) for x in parts}
-        mask_sb = new("mask_sb", [P, PACK, NQ], F32)
+        mask_sb = [new("mask_sb%d" % u, [P, PACK, HALF], F32) for u in range(2)]
         og_sb = [new("og_sb%d" % pair, [P, 2, NQ // COLS, E], F32) for pair in range(2)]
         gate = [new("gate%d" % h, [P, NQ // COLS, E], F32) for h in range(H)]
 
-        units = [(0, 0), (0, 1), (1, 0), (1, 1), (2, 0), (3, 0), (2, 1), (3, 1)]
+        units = [(2 * pair + g, u) for pair in range(2) for u in range(2) for g in range(2)]
         a_sb = [new("a_sb%d" % n, [P, PACK, HALF], F32) for n in range(len(units))]
         w_bf = [new("w_bf%d" % n, [P, HALF, PACK], BF16) for n in range(len(units))]
         w_codes = [new("w_codes%d" % n, [P, HALF], U32) for n in range(len(units))]
@@ -103,30 +103,29 @@ def tile_rows_a_lin_kb_mask_gate_kernel(tc, qT, kT, t, v, kb, mask, og, out):
         def quantize_q(x, cols=slice(0, HALF)):
             quantize(q_codes[x][:, cols], q_scales[x][:, cols], q_bf[x][:, cols, :].rearrange("p n j -> p (n j)"))
 
-        def scores(n):
-            h, u = units[n]
-            g = h % 2
-            rows = slice(g * ROWS, (g + 1) * ROWS)
-            x = (h // 2, u)
-            for i in range(2):
-                bank = score_psum.tile([P, 2, HALF], F32, name="scores_of_tile%d" % g)
-                banks[n, i] = bank
-                for r in range(2 * i, 2 * i + 2):
-                    tokens = slice(r * COLS, (r + 1) * COLS)
-                    for c in range(2):
+        def scores(*halves):
+            for n, i in halves:
+                banks[n, i] = score_psum.tile([P, 2, HALF], F32, name="scores_of_tile%d" % (units[n][0] % 2))
+            for place in range(2):
+                for c in range(2):
+                    for n, i in halves:
+                        h, u = units[n]
+                        rows = slice((h % 2) * ROWS, (h % 2 + 1) * ROWS)
+                        r = 2 * i + place
+                        tokens = slice(r * COLS, (r + 1) * COLS)
                         cols = slice(c * COLS, (c + 1) * COLS)
                         nc.tensor.matmul_mx(
-                            out=bank[:, r % 2, cols],
+                            out=banks[n, i][:, place, cols],
                             lhsT=k_codes[rows, tokens].bitcast(FP8X4),
                             lhsT_scale=k_scales[rows, tokens],
-                            rhs=q_codes[x][rows, cols].bitcast(FP8X4),
-                            rhs_scale=q_scales[x][rows, cols],
+                            rhs=q_codes[h // 2, u][rows, cols].bitcast(FP8X4),
+                            rhs_scale=q_scales[h // 2, u][rows, cols],
                             start=True,
                             stop=True,
                         )
 
-        def bias_and_scale(n):
-            for r in range(PACK):
+        def bias_and_scale(n, i):
+            for r in (2 * i, 2 * i + 1):
                 nc.scalar.activation(
                     out=a_sb[n][:, r, :],
                     in_=banks[n, r // 2][:, r % 2, :],
@@ -140,7 +139,7 @@ def tile_rows_a_lin_kb_mask_gate_kernel(tc, qT, kT, t, v, kb, mask, og, out):
             nc.vector.tensor_tensor(
                 out=runs_of_words(w_bf[n][:]),
                 in0=runs_of_rows(a_sb[n][:]),
-                in1=runs_of_rows(mask_sb[:, :, u * HALF : (u + 1) * HALF]),
+                in1=runs_of_rows(mask_sb[u][:]),
                 op=ALU.mult,
             )
 
@@ -187,7 +186,8 @@ def tile_rows_a_lin_kb_mask_gate_kernel(tc, qT, kT, t, v, kb, mask, og, out):
         nc.scalar.dma_start(out=kb_sb[:], in_=kb.rearrange("(p r) o -> p (r o)", r=PACK))
         nc.sync.dma_start(out=q_raw[0, 0], in_=q_rows(0)[:, :, 0:HALF])
         nc.sync.dma_start(out=q_raw[0, 1], in_=q_rows(0)[:, :, HALF:NQ])
-        nc.sync.dma_start(out=mask_sb[:], in_=mask.rearrange("(p r) n -> p r n", r=PACK))
+        mask_rows = mask.rearrange("(p r) n -> p r n", r=PACK)
+        nc.sync.dma_start(out=mask_sb[0][:], in_=mask_rows[:, :, 0:HALF])
 
         nc.vector.memset(k_mx[:, N : N + N // 4], 0)
         round_k(round_on_vector, 0)
@@ -201,61 +201,72 @@ def tile_rows_a_lin_kb_mask_gate_kernel(tc, qT, kT, t, v, kb, mask, og, out):
         quantize_k(3)
         nc.sync.dma_start(out=k_mx[ROWS:P, :].bitcast(I32), in_=k_mx[0:ROWS, :].bitcast(I32))
         nc.sync.dma_start(out=q_raw_late[:], in_=q_rows(1))
+        nc.sync.dma_start(out=mask_sb[1][:], in_=mask_rows[:, :, HALF:NQ])
         nc.sync.dma_start(out=v_raw[:], in_=v[0].rearrange("(p j) e -> p j e", j=PACK))
         load_og(0)
         load_og(1)
 
         quantize_q((0, 0), first)
         quantize_q((0, 0), second)
-        scores(0)
+        scores((0, 0))
+        scores((0, 1))
         round_q(round_on_vector, (0, 1))
-        bias_and_scale(0)
+        bias_and_scale(0, 0)
         quantize_q((0, 1))
-        scores(1)
-        bias_and_scale(1)
+        scores((1, 0), (2, 0))
+        bias_and_scale(0, 1)
         decay(0)
-        scores(2)
-        bias_and_scale(2)
-        decay(1)
-        scores(3)
+        scores((1, 1), (2, 1))
+        bias_and_scale(1, 0)
+        scores((3, 0))
+        bias_and_scale(1, 1)
+        round_q(round_on_vector, (1, 0))
         quantize_w(0)
-        round_q(round_on_scalar, (1, 0))
-        bias_and_scale(3)
-        decay(2)
         quantize_q((1, 0))
-        scores(4)
-        nc.vector.tensor_scalar_mul(runs_of_words(v_bf[:]), runs_of_rows(v_raw[:]), 1.0 / 32.0)
-        quantize_w(1)
+        decay(1)
+        bias_and_scale(2, 0)
+        scores((3, 1), (4, 0))
+        bias_and_scale(2, 1)
         round_q(round_on_scalar, (1, 1))
-        bias_and_scale(4)
-        decay(3)
+        decay(2)
+        nc.vector.tensor_scalar_mul(runs_of_words(v_bf[:]), runs_of_rows(v_raw[:]), 1.0 / 32.0)
+        bias_and_scale(3, 0)
+        scores((4, 1), (5, 0))
+        bias_and_scale(3, 1)
+        quantize_q((1, 1))
+        quantize_w(1)
         quantize(v_codes[:], v_scales[:], v_bf[:].rearrange("p e j -> p (e j)"))
-        scores(5)
         values(0)
         values(1)
-        quantize_q((1, 1))
+        decay(3)
+        bias_and_scale(4, 0)
+        scores((5, 1), (6, 0))
         quantize_w(2)
         values(2)
+        bias_and_scale(4, 1)
         gate_tanh(0)
-        bias_and_scale(5)
         decay(4)
-        scores(6)
-        finish(0)
+        bias_and_scale(5, 0)
+        scores((6, 1), (7, 0))
         quantize_w(3)
         values(3)
-        finish(1)
-        bias_and_scale(6)
+        bias_and_scale(5, 1)
+        finish(0)
+        finish(2)
         gate_tanh(1)
         decay(5)
-        scores(7)
+        bias_and_scale(6, 0)
+        scores((7, 1))
         quantize_w(4)
         values(4)
-        bias_and_scale(7)
-        decay(6)
-        finish(2)
+        bias_and_scale(6, 1)
+        finish(1)
         finish(3)
+        decay(6)
         quantize_w(5)
         values(5)
+        bias_and_scale(7, 0)
+        bias_and_scale(7, 1)
         gate_tanh(3)
         gate_tanh(2)
         decay(7)

from contextlib import ExitStack

import concourse.mybir as mybir

H, D, NQ, N, E = 4, 256, 512, 512, 128
FLOPS = 2 * H * N * NQ * D + 2 * H * NQ * N * E

F32 = mybir.dt.float32
BF16 = mybir.dt.bfloat16
U32 = mybir.dt.uint32
I32 = mybir.dt.int32
U8 = mybir.dt.uint8
FP8X4 = mybir.dt.float8_e4m3fn_x4
ACT = mybir.ActivationFunctionType
ALU = mybir.AluOpType

P = 128
PACK = 4
ROWS = D // PACK
COLS = 128
HALF = 256
RUN = 2


def tile_rows_a_lin_kb_mask_gate_kernel(tc, qT, kT, t, v, kb, mask, og, out):
    nc = tc.nc
    with ExitStack() as ctx:
        sb = ctx.enter_context(tc.tile_pool(name="sb", bufs=1))
        score_psum = ctx.enter_context(tc.psum_pool(name="score_psum", bufs=3))
        y_psum = ctx.enter_context(tc.psum_pool(name="y_psum", bufs=2))
        ctx.enter_context(tc.manual_schedule())

        def new(name, shape, dtype):
            return sb.tile(shape, dtype, name=name, align_bytes=64)

        t_sb = new("t_sb", [P, PACK], F32)
        kb_sb = new("kb_sb", [P, PACK], F32)
        kbt = new("kbt", [P, PACK], F32)
        k_raw = new("k_raw", [P, PACK, N], F32)
        k_bf = [new("k_bf%d" % i, [P, 2, COLS, PACK], BF16) for i in range(2)]
        k_mx = new("k_mx", [P, N + N // 4], U32)
        k_codes = k_mx[:, 0:N]
        k_scales = k_mx[:, N : N + N // 4].bitcast(U8)
        v_raw = new("v_raw", [P, PACK, E], F32)
        v_bf = new("v_bf", [P, E, PACK], BF16)
        v_codes = new("v_codes", [P, E], U32)
        v_scales = new("v_scales", [P, E], U8)
        parts = [(pair, u) for pair in range(2) for u in range(2)]
        q_raw = {(0, u): new("q_raw0%d" % u, [P, PACK, HALF], F32)[:] for u in range(2)}
        q_raw_late = new("q_raw_late", [P, PACK, NQ], F32)
        for u in range(2):
            q_raw[1, u] = q_raw_late[:, :, u * HALF : (u + 1) * HALF]
        q_bf = {x: new("q_bf%d%d" % x, [P, HALF, PACK], BF16) for x in parts}
        q_codes = {x: new("q_codes%d%d" % x, [P, HALF], U32) for x in parts}
        q_scales = {x: new("q_scales%d%d" % x, [P, HALF], U8) for x in parts}
        mask_sb = [new("mask_sb%d" % u, [P, PACK, HALF], F32) for u in range(2)]
        og_sb = [new("og_sb%d" % pair, [P, 2, NQ // COLS, E], F32) for pair in range(2)]
        gate = [new("gate%d" % h, [P, NQ // COLS, E], F32) for h in range(H)]

        units = [(2 * pair + g, u) for pair in range(2) for u in range(2) for g in range(2)]
        a_sb = [new("a_sb%d" % n, [P, PACK, HALF], F32) for n in range(len(units))]
        w_bf = [new("w_bf%d" % n, [P, HALF, PACK], BF16) for n in range(len(units))]
        w_codes = [new("w_codes%d" % n, [P, HALF], U32) for n in range(len(units))]
        w_scales = [new("w_scales%d" % n, [P, HALF], U8) for n in range(len(units))]
        o_sb = [new("o_sb%d" % n, [P, 2, E], F32) for n in range(len(units))]
        banks = {}
        y_bank = {}

        def runs_of_rows(ap):
            return ap.rearrange("p j (n i) -> p n j i", i=RUN)

        def runs_of_words(ap):
            return ap.rearrange("p (n i) j -> p n j i", i=RUN)

        def quantize(codes, scales, words):
            nc.vector.quantize_mx(out=codes.bitcast(FP8X4), scales=scales, in_=words)

        def q_rows(pair):
            return qT[2 * pair : 2 * pair + 2].rearrange("g (p j) n -> (g p) j n", j=PACK)

        def load_og(pair):
            rows = og[2 * pair : 2 * pair + 2].rearrange("g (c m) e -> m (g c) e", m=COLS)
            nc.sync.dma_start(out=og_sb[pair][:].rearrange("p g c e -> p (g c) e"), in_=rows)

        def round_on_vector(dst, src):
            nc.vector.tensor_copy(out=dst, in_=src)

        def round_on_scalar(dst, src):
            nc.scalar.activation(out=dst, in_=src, func=ACT.Copy)

        def round_k(rounder, i):
            src = k_raw[0:ROWS].rearrange("p j (m r) -> p m j r", r=PACK)[:, :, :, 2 * i : 2 * i + 2]
            rounder(k_bf[i][0:ROWS].rearrange("p r m j -> p m j r"), src)

        def quantize_k(r):
            cols = slice(r * COLS, (r + 1) * COLS)
            words = k_bf[r // 2][0:ROWS, r % 2].rearrange("p m j -> p (m j)")
            quantize(k_codes[0:ROWS, cols], k_scales[0:ROWS, cols], words)

        def round_q(rounder, x, cols=slice(0, HALF)):
            rounder(runs_of_words(q_bf[x][:, cols, :]), runs_of_rows(q_raw[x][:, :, cols]))

        def quantize_q(x, cols=slice(0, HALF)):
            quantize(q_codes[x][:, cols], q_scales[x][:, cols], q_bf[x][:, cols, :].rearrange("p n j -> p (n j)"))

        def scores(*halves):
            for n, i in halves:
                banks[n, i] = score_psum.tile([P, 2, HALF], F32, name="scores_of_tile%d" % (units[n][0] % 2))
            for place in range(2):
                for c in range(2):
                    for n, i in halves:
                        h, u = units[n]
                        rows = slice((h % 2) * ROWS, (h % 2 + 1) * ROWS)
                        r = 2 * i + place
                        tokens = slice(r * COLS, (r + 1) * COLS)
                        cols = slice(c * COLS, (c + 1) * COLS)
                        nc.tensor.matmul_mx(
                            out=banks[n, i][:, place, cols],
                            lhsT=k_codes[rows, tokens].bitcast(FP8X4),
                            lhsT_scale=k_scales[rows, tokens],
                            rhs=q_codes[h // 2, u][rows, cols].bitcast(FP8X4),
                            rhs_scale=q_scales[h // 2, u][rows, cols],
                            start=True,
                            stop=True,
                        )

        def bias_and_scale(n, i):
            for r in (2 * i, 2 * i + 1):
                nc.scalar.activation(
                    out=a_sb[n][:, r, :],
                    in_=banks[n, r // 2][:, r % 2, :],
                    func=ACT.Identity,
                    bias=kbt[:, r : r + 1],
                    scale=t_sb[:, r : r + 1],
                )

        def decay(n):
            u = units[n][1]
            nc.vector.tensor_tensor(
                out=runs_of_words(w_bf[n][:]),
                in0=runs_of_rows(a_sb[n][:]),
                in1=runs_of_rows(mask_sb[u][:]),
                op=ALU.mult,
            )

        def quantize_w(n):
            quantize(w_codes[n][:], w_scales[n][:], w_bf[n][:].rearrange("p n r -> p (n r)"))

        def values(n):
            h, u = units[n]
            if u == 0:
                y_bank[h] = y_psum.tile([P, NQ // COLS, E], F32, name="y_bank")
            for c in range(2):
                cols = slice(c * COLS, (c + 1) * COLS)
                nc.tensor.matmul_mx(
                    out=y_bank[h][:, 2 * u + c, :],
                    lhsT=w_codes[n][:, cols].bitcast(FP8X4),
                    lhsT_scale=w_scales[n][:, cols],
                    rhs=v_codes[:].bitcast(FP8X4),
                    rhs_scale=v_scales[:],
                    start=True,
                    stop=True,
                )

        def gate_tanh(h):
            nc.scalar.activation(out=gate[h][:], in_=og_sb[h // 2][:, h % 2], func=ACT.Tanh, scale=0.5)

        def finish(n):
            h, u = units[n]
            tiles = slice(2 * u, 2 * u + 2)
            nc.vector.scalar_tensor_tensor(
                out=o_sb[n][:],
                in0=gate[h][:, tiles, :],
                scalar=1.0,
                in1=y_bank[h][:, tiles, :],
                op0=ALU.add,
                op1=ALU.mult,
            )
            rows = out[h].rearrange("(c m) e -> m c e", m=COLS)
            nc.sync.dma_start(out=rows[:, tiles, :], in_=o_sb[n][:])

        first, second = slice(0, COLS), slice(COLS, HALF)

        nc.sync.dma_start(out=k_raw[0:ROWS], in_=kT[0].rearrange("(p j) n -> p j n", j=PACK))
        nc.scalar.dma_start(out=t_sb[:], in_=t.rearrange("(p r) o -> p (r o)", r=PACK))
        nc.scalar.dma_start(out=kb_sb[:], in_=kb.rearrange("(p r) o -> p (r o)", r=PACK))
        nc.sync.dma_start(out=q_raw[0, 0], in_=q_rows(0)[:, :, 0:HALF])
        nc.sync.dma_start(out=q_raw[0, 1], in_=q_rows(0)[:, :, HALF:NQ])
        mask_rows = mask.rearrange("(p r) n -> p r n", r=PACK)
        nc.sync.dma_start(out=mask_sb[0][:], in_=mask_rows[:, :, 0:HALF])

        nc.vector.memset(k_mx[:, N : N + N // 4], 0)
        round_k(round_on_vector, 0)
        round_k(round_on_scalar, 1)
        nc.vector.tensor_tensor(out=kbt[:], in0=kb_sb[:], in1=t_sb[:], op=ALU.mult)
        quantize_k(0)
        quantize_k(1)
        round_q(round_on_vector, (0, 0), first)
        round_q(round_on_scalar, (0, 0), second)
        quantize_k(2)
        quantize_k(3)
        nc.sync.dma_start(out=k_mx[ROWS:P, :].bitcast(I32), in_=k_mx[0:ROWS, :].bitcast(I32))
        nc.sync.dma_start(out=q_raw_late[:], in_=q_rows(1))
        nc.sync.dma_start(out=mask_sb[1][:], in_=mask_rows[:, :, HALF:NQ])
        nc.sync.dma_start(out=v_raw[:], in_=v[0].rearrange("(p j) e -> p j e", j=PACK))
        load_og(0)
        load_og(1)

        quantize_q((0, 0), first)
        quantize_q((0, 0), second)
        scores((0, 0))
        scores((0, 1))
        round_q(round_on_vector, (0, 1))
        bias_and_scale(0, 0)
        quantize_q((0, 1))
        scores((1, 0), (2, 0))
        bias_and_scale(0, 1)
        decay(0)
        scores((1, 1), (2, 1))
        bias_and_scale(1, 0)
        scores((3, 0))
        bias_and_scale(1, 1)
        round_q(round_on_vector, (1, 0))
        quantize_w(0)
        quantize_q((1, 0))
        decay(1)
        bias_and_scale(2, 0)
        scores((3, 1), (4, 0))
        bias_and_scale(2, 1)
        round_q(round_on_scalar, (1, 1))
        decay(2)
        nc.vector.tensor_scalar_mul(runs_of_words(v_bf[:]), runs_of_rows(v_raw[:]), 1.0 / 32.0)
        bias_and_scale(3, 0)
        scores((4, 1), (5, 0))
        bias_and_scale(3, 1)
        quantize_q((1, 1))
        quantize_w(1)
        quantize(v_codes[:], v_scales[:], v_bf[:].rearrange("p e j -> p (e j)"))
        values(0)
        values(1)
        decay(3)
        bias_and_scale(4, 0)
        scores((5, 1), (6, 0))
        quantize_w(2)
        values(2)
        bias_and_scale(4, 1)
        gate_tanh(0)
        decay(4)
        bias_and_scale(5, 0)
        scores((6, 1), (7, 0))
        quantize_w(3)
        values(3)
        bias_and_scale(5, 1)
        finish(0)
        finish(2)
        gate_tanh(1)
        decay(5)
        bias_and_scale(6, 0)
        scores((7, 1))
        quantize_w(4)
        values(4)
        bias_and_scale(6, 1)
        finish(1)
        finish(3)
        decay(6)
        quantize_w(5)
        values(5)
        bias_and_scale(7, 0)
        bias_and_scale(7, 1)
        gate_tanh(3)
        gate_tanh(2)
        decay(7)
        quantize_w(6)
        values(6)
        finish(5)
        quantize_w(7)
        values(7)
        finish(4)
        finish(6)
        finish(7)
